import numpy as np
import ml_dtypes


def mxq(x, axis, fmt="e4m3"):
    dtype, down = {"e4m3": (ml_dtypes.float8_e4m3fn, 7), "e5m2": (ml_dtypes.float8_e5m2, 14)}[fmt]
    v = np.moveaxis(np.asarray(x, np.float32).astype(ml_dtypes.bfloat16).astype(np.float64), axis, -1)
    blocks = v.reshape(v.shape[:-1] + (-1, 32))
    amax = np.abs(blocks).max(-1, keepdims=True)
    byte = np.maximum(np.where(amax > 0, np.frexp(amax)[1] - 1 + 127, 0) - down, 1)
    scale = np.exp2(byte - 127.0)
    codes = (blocks / scale).astype(np.float32).astype(dtype).astype(np.float64)
    return np.moveaxis((codes * scale).reshape(v.shape), -1, axis)


WIDE = False


def mx_kscale(k):
    if not WIDE:
        return np.ones(k)
    levels = np.array([30, -30])
    if k % 512:
        return np.exp2(np.random.permutation(np.resize(levels, k // 32))).repeat(32)
    a = np.empty((k // 512, 16))
    for p in range(k // 512):
        a[p, :8] = np.random.permutation(np.resize(levels, 8))
        for g in range(8):
            far = levels[np.abs(levels - a[p, g]) >= 10]
            a[p, g + 8] = far[np.random.randint(len(far))]
    return np.exp2(a.ravel()).repeat(32)


def f64(x):
    return np.asarray(x).astype(np.float64)


def striped(idx):
    return np.tile(np.asarray(idx).reshape(-1, 16).T, (8, 1)).astype(np.uint16)


def unstriped(offs):
    return offs[:16].T.reshape(-1).astype(np.int64)


E2M1 = np.array([0.0, 0.5, 1.0, 1.5, 2.0, 3.0, 4.0, 6.0, -0.0, -0.5, -1.0, -1.5, -2.0, -3.0, -4.0, -6.0])


def pack_weight(w, fmt):
    k, n = w.shape
    w = f64(np.asarray(w, np.float32).astype(ml_dtypes.bfloat16)).reshape(k // 32, 32, n)
    amax = np.abs(w).max(1)
    if fmt in ("e4m3", "e5m2"):
        byte = np.frexp(amax)[1] - 1 + 127 - (7 if fmt == "e4m3" else 14)
    else:
        mant, ex = np.frexp(amax / 6.0)
        byte = np.where(mant > 0.5, ex, ex - 1) + 127
    byte = np.clip(np.where(amax > 0, byte, 1), 1, 254)
    scaled = (w * np.exp2(127.0 - byte)[:, None, :]).reshape(k, n).astype(np.float32)
    by_word = np.ascontiguousarray(scaled.reshape(k // 512, 128, 4, n).transpose(0, 1, 3, 2))
    if fmt in ("e4m3", "e5m2"):
        words = by_word.astype(ml_dtypes.float8_e4m3fn if fmt == "e4m3" else ml_dtypes.float8_e5m2).view(np.uint8)
    else:
        c = by_word.astype(ml_dtypes.float4_e2m1fn).view(np.uint8) & 0xF
        words = (c[..., 0::2] | (c[..., 1::2] << 4)).reshape(k // 512, 128, 2 * n)
    return np.ascontiguousarray(words), np.ascontiguousarray(byte.astype(np.uint8).reshape(k // 512, 16, n))


def unpack_weight(words, scales, fmt):
    g, _, n = scales.shape
    words = np.ascontiguousarray(words).reshape(g, 128, n, -1)
    if fmt in ("e4m3", "e5m2"):
        vals = words.view(ml_dtypes.float8_e4m3fn if fmt == "e4m3" else ml_dtypes.float8_e5m2).astype(np.float64)
    else:
        nib = np.empty((g, 128, n, 4), np.uint8)
        nib[..., 0::2] = words & 0xF
        nib[..., 1::2] = words >> 4
        vals = E2M1[nib]
    vals = vals * np.repeat(np.exp2(scales.astype(np.float64) - 127.0), 8, axis=1)[..., None]
    return vals.transpose(0, 1, 3, 2).reshape(g * 512, n)


K, T, J, I, V, G = 1024, 1024, 256, 256, 1024, 32


def setup_inputs():
    n = np.random.standard_normal
    idx = np.random.permutation(T)[:J]
    idx2 = np.random.permutation(T)[:J]
    idx3 = np.random.permutation(V)[:I]
    fk = mx_kscale(K)
    kyp = pack_weight(n((K, V)) / fk[:, None], "e5m2")
    return {
        "xf": (n((K, T)) * 0.03).astype(np.float32),
        "fk": (np.random.uniform(0.5, 2.0, (K, 1)) * fk[:, None]).astype(np.float32),
        "ky_words": kyp[0],
        "ky_scales": kyp[1],
        "bi": (np.random.uniform(-0.7, 0.7, (1, I))).astype(np.float32),
        "offs": striped(idx),
        "offs2": striped(idx2),
        "offs3": striped(idx3),
    }


def reference(xf, fk, ky_words, ky_scales, bi, offs, offs2, offs3):
    idx = unstriped(offs)
    idx2 = unstriped(offs2)
    idx3 = unstriped(offs3)
    kyu = unpack_weight(ky_words, ky_scales, "e5m2")
    u = (f64(xf)[:, idx] - f64(xf)[:, idx2]) * f64(fk)
    uq = mxq(u, 0, "e5m2")
    kyidx3g = kyu[:, idx3]
    a0 = uq.T @ kyidx3g
    a = a0 + f64(bi)
    g1 = a.reshape(J, G, I // G).max(axis=2)
    y = g1 - 0.5 * np.max(a, axis=1, keepdims=True)
    return y

@@ -1,0 +1,184 @@
+from contextlib import ExitStack
+
+import concourse.mybir as mybir
+from concourse.masks import make_identity
+
+K, T, J, I, V, G = 1024, 1024, 256, 256, 1024, 32
+FLOPS = 2 * K * J * I
+
+F32 = mybir.dt.float32
+BF16 = mybir.dt.bfloat16
+I32 = mybir.dt.int32
+U32 = mybir.dt.uint32
+U16 = mybir.dt.uint16
+U8 = mybir.dt.uint8
+E5M2X4 = mybir.dt.float8_e5m2_x4
+ALU = mybir.AluOpType
+COPY = mybir.ActivationFunctionType.Copy
+AXIS_X = mybir.AxisListType.X
+
+P = 128
+PACK = 4
+PASSES = K // (P * PACK)
+HALF = 128
+LIST_COLS = HALF // 16
+
+
+def tile_list_scores_gaps_listed_bundles_kernel(tc, xf, fk, ky_words, ky_scales, bi, offs, offs2, offs3, out):
+    nc = tc.nc
+    with ExitStack() as ctx:
+        keep = ctx.enter_context(tc.tile_pool(name="keep", bufs=1))
+        psum = ctx.enter_context(tc.psum_pool(name="psum", bufs=1))
+
+        def tile(shape, dtype, name):
+            return keep.tile(shape, dtype, name=name, align_bytes=64)
+
+        list1 = keep.tile([P, J // 16], U16, name="list1")
+        list2 = keep.tile([P, J // 16], U16, name="list2")
+        list3 = keep.tile([P, I // 16], U16, name="list3")
+        planes = [[tile([P, T], F32, f"x{a}{t}") for t in range(PACK)] for a in range(PASSES)]
+        key_words = [tile([P, V], I32, f"kw{a}") for a in range(PASSES)]
+        key_scales = tile([P, PASSES * V], U8, "ks")
+        factor0 = tile([P, PACK], F32, "factor0")
+        factor1_lo = tile([P, 2], F32, "factor1_lo")
+        factor1_hi = tile([P, 2], F32, "factor1_hi")
+        bias_col = tile([P, 2], F32, "bias_col")
+        ident = tile([P, P], F32, "ident")
+        bias = tile([P, I], F32, "bias")
+
+        xf_planes = xf.rearrange("(a p t) c -> a t p c", a=PASSES, t=PACK)
+
+        def load_plane(a, t):
+            nc.sync.dma_start(out=planes[a][t][:], in_=xf_planes[a, t])
+
+        def load_scale_rows(q):
+            nc.sync.dma_start(
+                out=key_scales[32 * q : 32 * q + 4, :].bitcast(I32).rearrange("r (a c) -> r a c", a=PASSES),
+                in_=ky_scales[:, 4 * q : 4 * q + 4, :].bitcast(I32).rearrange("a r c -> r a c"),
+            )
+
+        def load_words(a):
+            nc.sync.dma_start(out=key_words[a][:], in_=ky_words[a].rearrange("p n t -> p (n t)").bitcast(I32))
+
+        nc.vector.memset(key_scales[:].bitcast(I32), 0)
+        fk_rows = fk.rearrange("(a p t) o -> a p (t o)", a=PASSES, t=PACK)
+        nc.gpsimd.dma_start(out=bias_col[:], in_=bi.rearrange("o (p c) -> p (o c)", c=2))
+        nc.gpsimd.dma_start(out=factor1_lo[:], in_=fk_rows[1][:, 0:2])
+        make_identity(nc, ident[:])
+
+        load_plane(0, 0)
+        nc.sync.dma_start(list2[:], offs2)
+        nc.sync.dma_start(list1[:], offs)
+        load_plane(0, 1)
+        nc.sync.dma_start(list3[:], offs3)
+        load_scale_rows(0)
+        load_scale_rows(1)
+        load_plane(0, 2)
+        load_scale_rows(2)
+        load_scale_rows(3)
+        load_plane(0, 3)
+        load_plane(1, 0)
+        nc.sync.dma_start(out=factor0[:], in_=fk_rows[0])
+        for t in range(1, PACK):
+            load_plane(1, t)
+        nc.sync.dma_start(out=factor1_hi[:], in_=fk_rows[1][:, 2:4])
+        load_words(0)
+        load_words(1)
+
+        bias_ps = psum.tile([P, 2, P], F32, name="bias_ps")
+        for c in range(2):
+            nc.tensor.transpose(bias_ps[:, c, :], bias_col[:, c : c + 1].to_broadcast([P, P]), ident[:])
+        nc.vector.tensor_copy(out=bias[:].rearrange("m (p c) -> m p c", c=2), in_=bias_ps[:].rearrange("m c p -> m p c"))
+
+        woven = [tile([P, J, PACK], BF16, f"woven{a}") for a in range(PASSES)]
+        flat0 = tile([P, PACK, J], BF16, "flat0")
+        u_codes = [tile([P, J], U32, f"uc{a}") for a in range(PASSES)]
+        u_scales = [tile([P, J], U8, f"us{a}") for a in range(PASSES)]
+        k_codes = [[tile([P, HALF], U32, f"kc{a}{h}") for h in range(2)] for a in range(PASSES)]
+        k_scales = [tile([P, I], U8, f"ksg{a}") for a in range(PASSES)]
+        acc = [psum.tile([P, 2, HALF], F32, name=f"acc{h}") for h in range(2)]
+
+        def gap(a, t, j0, n):
+            second = tile([P, n], F32, f"second{a}{t}{j0}")
+            diff = tile([P, n], F32, f"diff{a}{t}{j0}")
+            cols = slice(j0 // 16, (j0 + n) // 16)
+            nc.scalar.activation(second[:], planes[a][t][:].indirect(list2[:, cols]), COPY)
+            nc.vector.tensor_tensor(diff[:], planes[a][t][:].indirect(list1[:, cols]), second[:], ALU.subtract)
+            return diff
+
+        def quantise(a, j0, n):
+            nc.vector.quantize_mx(
+                out=u_codes[a][:, j0 : j0 + n].bitcast(E5M2X4),
+                scales=u_scales[a][:, j0 : j0 + n],
+                in_=woven[a][:, j0 : j0 + n, :].rearrange("p j t -> p (j t)"),
+            )
+
+        def gather_words(a, h):
+            nc.vector.tensor_copy(k_codes[a][h][:], key_words[a][:].bitcast(U32).indirect(list3[:, h * LIST_COLS : (h + 1) * LIST_COLS]))
+
+        def multiply(a, h):
+            for jh in range(2):
+                rows = slice(jh * HALF, (jh + 1) * HALF)
+                nc.tensor.matmul_mx(
+                    out=acc[h][:, jh, :],
+                    lhsT=u_codes[a][:, rows].bitcast(E5M2X4),
+                    lhsT_scale=u_scales[a][:, rows],
+                    rhs=k_codes[a][h][:].bitcast(E5M2X4),
+                    rhs_scale=k_scales[a][:, h * HALF : (h + 1) * HALF],
+                    start=(a == 0 and jh == 0),
+                    stop=(a == PASSES - 1 and jh == 1),
+                )
+
+        diffs0 = []
+        for t in range(PACK):
+            diffs0.append(gap(0, t, 0, J))
+            if t == 2:
+                for a in range(PASSES):
+                    nc.vector.tensor_copy(k_scales[a][:], key_scales[:, a * V : (a + 1) * V].indirect(list3[:]))
+        for t in range(2):
+            diff = gap(1, t, 0, J)
+            if t == 0:
+                for s in range(PACK):
+                    nc.scalar.activation(flat0[:, s, :], diffs0[s][:], COPY, scale=factor0[:, s : s + 1])
+            if t == 1:
+                nc.vector.tensor_copy(
+                    out=woven[0][:].rearrange("p (c i) t -> p c t i", i=4),
+                    in_=flat0[:].rearrange("p t (c i) -> p c t i", i=4),
+                )
+            nc.vector.tensor_scalar(woven[1][:, :, t], diff[:], factor1_lo[:, t : t + 1], None, ALU.mult)
+            if t == 1:
+                quantise(0, 0, J)
+        diff2 = gap(1, 2, 0, J)
+        last = [gap(1, 3, jh * HALF, HALF) for jh in range(2)]
+        nc.scalar.activation(woven[1][:, :, 2], diff2[:], COPY, scale=factor1_hi[:, 0:1])
+        for jh in range(2):
+            nc.scalar.activation(woven[1][:, jh * HALF : (jh + 1) * HALF, 3], last[jh][:], COPY, scale=factor1_hi[:, 1:2])
+        for h in range(2):
+            gather_words(0, h)
+            multiply(0, h)
+        for jh in range(2):
+            quantise(1, jh * HALF, HALF)
+        for h in range(2):
+            gather_words(1, h)
+            multiply(1, h)
+
+        scores = [tile([P, 2, HALF], F32, f"scores{h}") for h in range(2)]
+        bundle = tile([P, 2, G], F32, "bundle")
+        row_max = tile([P, 2], F32, "row_max")
+        result = tile([P, 2, G], F32, "result")
+        for h in range(2):
+            nc.vector.tensor_tensor(
+                scores[h][:], acc[h][:], bias[:, h * HALF : (h + 1) * HALF].unsqueeze(1).to_broadcast([P, 2, HALF]), ALU.add
+            )
+        for h in range(2):
+            nc.vector.tensor_reduce(
+                bundle[:, :, h * (G // 2) : (h + 1) * (G // 2)],
+                scores[h][:].rearrange("p j (g e) -> p j g e", e=I // G),
+                AXIS_X,
+                ALU.max,
+            )
+        nc.vector.tensor_reduce(row_max[:], bundle[:], AXIS_X, ALU.max)
+        nc.vector.scalar_tensor_tensor(
+            result[:], row_max[:].unsqueeze(2).to_broadcast([P, 2, G]), -0.5, bundle[:], ALU.mult, ALU.add
+        )
+        nc.sync.dma_start(out=out.rearrange("(h p) g -> p h g", p=P), in_=result[:])

@@ -39,9 +39,7 @@ def tile_list_scores_gaps_listed_bundles_kernel(tc, xf, fk, ky_words, ky_scales,
         planes = [[tile([P, T], F32, f"x{a}{t}") for t in range(PACK)] for a in range(PASSES)]
         key_words = [tile([P, V], I32, f"kw{a}") for a in range(PASSES)]
         key_scales = tile([P, PASSES * V], U8, "ks")
-        factor0 = tile([P, PACK], F32, "factor0")
-        factor1_lo = tile([P, 2], F32, "factor1_lo")
-        factor1_hi = tile([P, 2], F32, "factor1_hi")
+        factor = [[tile([P, 2], F32, f"factor{a}{u}") for u in range(2)] for a in range(PASSES)]
         bias_col = tile([P, 2], F32, "bias_col")
         ident = tile([P, P], F32, "ident")
         bias = tile([P, I], F32, "bias")
@@ -60,123 +58,139 @@ def tile_list_scores_gaps_listed_bundles_kernel(tc, xf, fk, ky_words, ky_scales,
         def load_words(a):
             nc.sync.dma_start(out=key_words[a][:], in_=ky_words[a].rearrange("p n t -> p (n t)").bitcast(I32))
 
+        warm = tile([P, 1], F32, "warm")
+        nc.vector.memset(warm[:], 0.0)
+        warm2 = tile([P, 1], F32, "warm2")
+        nc.scalar.activation(warm2[:], warm[:], COPY)
         nc.vector.memset(key_scales[:].bitcast(I32), 0)
         fk_rows = fk.rearrange("(a p t) o -> a p (t o)", a=PASSES, t=PACK)
-        nc.gpsimd.dma_start(out=bias_col[:], in_=bi.rearrange("o (p c) -> p (o c)", c=2))
-        nc.gpsimd.dma_start(out=factor1_lo[:], in_=fk_rows[1][:, 0:2])
         make_identity(nc, ident[:])
 
         load_plane(0, 0)
         nc.sync.dma_start(list2[:], offs2)
         nc.sync.dma_start(list1[:], offs)
         load_plane(0, 1)
-        nc.sync.dma_start(list3[:], offs3)
+        nc.sync.dma_start(out=bias_col[:], in_=bi.rearrange("o (p c) -> p (o c)", c=2))
         load_scale_rows(0)
         load_scale_rows(1)
         load_plane(0, 2)
+        nc.sync.dma_start(list3[:], offs3)
         load_scale_rows(2)
         load_scale_rows(3)
         load_plane(0, 3)
+        nc.sync.dma_start(out=factor[0][0][:], in_=fk_rows[0][:, 0:2])
         load_plane(1, 0)
-        nc.sync.dma_start(out=factor0[:], in_=fk_rows[0])
-        for t in range(1, PACK):
-            load_plane(1, t)
-        nc.sync.dma_start(out=factor1_hi[:], in_=fk_rows[1][:, 2:4])
+        nc.sync.dma_start(out=factor[0][1][:], in_=fk_rows[0][:, 2:4])
+        load_plane(1, 1)
+        load_plane(1, 2)
+        nc.sync.dma_start(out=factor[1][0][:], in_=fk_rows[1][:, 0:2])
+        load_plane(1, 3)
         load_words(0)
+        nc.sync.dma_start(out=factor[1][1][:], in_=fk_rows[1][:, 2:4])
         load_words(1)
 
         bias_ps = psum.tile([P, 2, P], F32, name="bias_ps")
         for c in range(2):
             nc.tensor.transpose(bias_ps[:, c, :], bias_col[:, c : c + 1].to_broadcast([P, P]), ident[:])
-        nc.vector.tensor_copy(out=bias[:].rearrange("m (p c) -> m p c", c=2), in_=bias_ps[:].rearrange("m c p -> m p c"))
 
-        woven = [tile([P, J, PACK], BF16, f"woven{a}") for a in range(PASSES)]
-        flat0 = tile([P, PACK, J], BF16, "flat0")
+        flat = [tile([P, PACK, J], BF16, f"flat{a}") for a in range(PASSES)]
         u_codes = [tile([P, J], U32, f"uc{a}") for a in range(PASSES)]
         u_scales = [tile([P, J], U8, f"us{a}") for a in range(PASSES)]
-        k_codes = [[tile([P, HALF], U32, f"kc{a}{h}") for h in range(2)] for a in range(PASSES)]
+        k_codes = [tile([P, I], U32, f"kc{a}") for a in range(PASSES)]
         k_scales = [tile([P, I], U8, f"ksg{a}") for a in range(PASSES)]
-        acc = [psum.tile([P, 2, HALF], F32, name=f"acc{h}") for h in range(2)]
+        acc = [psum.tile([P, I], F32, name=f"acc{h}") for h in range(2)]
 
-        def gap(a, t, j0, n):
+        def gap(a, t, j0, n, first_on=None):
             second = tile([P, n], F32, f"second{a}{t}{j0}")
             diff = tile([P, n], F32, f"diff{a}{t}{j0}")
             cols = slice(j0 // 16, (j0 + n) // 16)
-            nc.scalar.activation(second[:], planes[a][t][:].indirect(list2[:, cols]), COPY)
-            nc.vector.tensor_tensor(diff[:], planes[a][t][:].indirect(list1[:, cols]), second[:], ALU.subtract)
+            window = planes[a][t][:]
+            nc.scalar.activation(second[:], window.indirect(list2[:, cols]), COPY)
+            if first_on is None:
+                nc.vector.tensor_tensor(diff[:], window.indirect(list1[:, cols]), second[:], ALU.subtract)
+                return diff
+            first = tile([P, n], F32, f"first{a}{t}{j0}")
+            if first_on == "vector":
+                nc.vector.tensor_copy(first[:], window.indirect(list1[:, cols]))
+            else:
+                nc.scalar.activation(first[:], window.indirect(list1[:, cols]), COPY)
+            nc.vector.tensor_tensor(diff[:], first[:], second[:], ALU.subtract)
             return diff
 
-        def quantise(a, j0, n):
+        def scale_on_vector(a, t, diff):
+            nc.vector.tensor_scalar(flat[a][:, t, :], diff[:], factor[a][t // 2][:, t % 2 : t % 2 + 1], None, ALU.mult)
+
+        def scale_on_scalar(a, t, diff, j0, n):
+            nc.scalar.activation(flat[a][:, t, j0 : j0 + n], diff[:], COPY, scale=factor[a][t // 2][:, t % 2 : t % 2 + 1])
+
+        def weave(copy, a, j0, n):
+            woven = tile([P, n, PACK], BF16, f"woven{a}{j0}")
+            copy(
+                out=woven[:].rearrange("p (c i) t -> p c t i", i=4),
+                in_=flat[a][:, :, j0 : j0 + n].rearrange("p t (c i) -> p c t i", i=4),
+            )
+            return woven
+
+        def quantise(a, woven, j0, n):
             nc.vector.quantize_mx(
                 out=u_codes[a][:, j0 : j0 + n].bitcast(E5M2X4),
                 scales=u_scales[a][:, j0 : j0 + n],
-                in_=woven[a][:, j0 : j0 + n, :].rearrange("p j t -> p (j t)"),
+                in_=woven[:].rearrange("p j t -> p (j t)"),
             )
 
-        def gather_words(a, h):
-            nc.vector.tensor_copy(k_codes[a][h][:], key_words[a][:].bitcast(U32).indirect(list3[:, h * LIST_COLS : (h + 1) * LIST_COLS]))
+        def multiply(a, jh):
+            rows = slice(jh * HALF, (jh + 1) * HALF)
+            nc.tensor.matmul_mx(
+                out=acc[jh][:],
+                lhsT=u_codes[a][:, rows].bitcast(E5M2X4),
+                lhsT_scale=u_scales[a][:, rows],
+                rhs=k_codes[a][:].bitcast(E5M2X4),
+                rhs_scale=k_scales[a][:],
+                start=(a == 0),
+                stop=(a == PASSES - 1),
+            )
 
-        def multiply(a, h):
-            for jh in range(2):
-                rows = slice(jh * HALF, (jh + 1) * HALF)
-                nc.tensor.matmul_mx(
-                    out=acc[h][:, jh, :],
-                    lhsT=u_codes[a][:, rows].bitcast(E5M2X4),
-                    lhsT_scale=u_scales[a][:, rows],
-                    rhs=k_codes[a][h][:].bitcast(E5M2X4),
-                    rhs_scale=k_scales[a][:, h * HALF : (h + 1) * HALF],
-                    start=(a == 0 and jh == 0),
-                    stop=(a == PASSES - 1 and jh == 1),
-                )
+        def gather_words(a):
+            nc.vector.tensor_copy(k_codes[a][:], key_words[a][:].bitcast(U32).indirect(list3[:]))
 
-        diffs0 = []
-        for t in range(PACK):
-            diffs0.append(gap(0, t, 0, J))
-            if t == 2:
-                for a in range(PASSES):
-                    nc.vector.tensor_copy(k_scales[a][:], key_scales[:, a * V : (a + 1) * V].indirect(list3[:]))
-        for t in range(2):
-            diff = gap(1, t, 0, J)
-            if t == 0:
-                for s in range(PACK):
-                    nc.scalar.activation(flat0[:, s, :], diffs0[s][:], COPY, scale=factor0[:, s : s + 1])
-            if t == 1:
-                nc.vector.tensor_copy(
-                    out=woven[0][:].rearrange("p (c i) t -> p c t i", i=4),
-                    in_=flat0[:].rearrange("p t (c i) -> p c t i", i=4),
-                )
-            nc.vector.tensor_scalar(woven[1][:, :, t], diff[:], factor1_lo[:, t : t + 1], None, ALU.mult)
-            if t == 1:
-                quantise(0, 0, J)
-        diff2 = gap(1, 2, 0, J)
-        last = [gap(1, 3, jh * HALF, HALF) for jh in range(2)]
-        nc.scalar.activation(woven[1][:, :, 2], diff2[:], COPY, scale=factor1_hi[:, 0:1])
+        d00 = gap(0, 0, 0, J, "vector")
+        nc.scalar.copy(out=bias[:].rearrange("m (p c) -> m p c", c=2), in_=bias_ps[:].rearrange("m c p -> m p c"))
+        d01 = gap(0, 1, 0, J)
+        for a in range(PASSES):
+            nc.vector.tensor_copy(k_scales[a][:], key_scales[:, a * V : (a + 1) * V].indirect(list3[:]))
+        scale_on_vector(0, 0, d00)
+        d02 = gap(0, 2, 0, J, "scalar")
+        scale_on_vector(0, 1, d01)
+        d03 = gap(0, 3, 0, J)
+        d10 = gap(1, 0, 0, J)
+        scale_on_scalar(0, 2, d02, 0, J)
+        scale_on_scalar(0, 3, d03, 0, J)
+        quantise(0, weave(nc.vector.tensor_copy, 0, 0, J), 0, J)
+        d11 = gap(1, 1, 0, J)
+        d12 = gap(1, 2, 0, J)
+        scale_on_scalar(1, 0, d10, 0, J)
+        scale_on_scalar(1, 1, d11, 0, J)
+        d13 = [gap(1, 3, jh * HALF, HALF) for jh in range(2)]
+        scale_on_scalar(1, 2, d12, 0, J)
         for jh in range(2):
-            nc.scalar.activation(woven[1][:, jh * HALF : (jh + 1) * HALF, 3], last[jh][:], COPY, scale=factor1_hi[:, 1:2])
-        for h in range(2):
-            gather_words(0, h)
-            multiply(0, h)
+            scale_on_scalar(1, 3, d13[jh], jh * HALF, HALF)
+        gather_words(0)
         for jh in range(2):
-            quantise(1, jh * HALF, HALF)
-        for h in range(2):
-            gather_words(1, h)
-            multiply(1, h)
+            multiply(0, jh)
+        woven1 = [weave(nc.vector.tensor_copy, 1, 0, HALF), weave(nc.scalar.copy, 1, HALF, HALF)]
+        gather_words(1)
+        for jh in range(2):
+            quantise(1, woven1[jh], jh * HALF, HALF)
+            multiply(1, jh)
 
-        scores = [tile([P, 2, HALF], F32, f"scores{h}") for h in range(2)]
+        scores = [tile([P, I], F32, f"scores{h}") for h in range(2)]
         bundle = tile([P, 2, G], F32, "bundle")
         row_max = tile([P, 2], F32, "row_max")
         result = tile([P, 2, G], F32, "result")
-        for h in range(2):
-            nc.vector.tensor_tensor(
-                scores[h][:], acc[h][:], bias[:, h * HALF : (h + 1) * HALF].unsqueeze(1).to_broadcast([P, 2, HALF]), ALU.add
-            )
-        for h in range(2):
-            nc.vector.tensor_reduce(
-                bundle[:, :, h * (G // 2) : (h + 1) * (G // 2)],
-                scores[h][:].rearrange("p j (g e) -> p j g e", e=I // G),
-                AXIS_X,
-                ALU.max,
-            )
+        for jh in range(2):
+            nc.vector.tensor_tensor(scores[jh][:], acc[jh][:], bias[:], ALU.add)
+        for jh in range(2):
+            nc.vector.tensor_reduce(bundle[:, jh, :], scores[jh][:].rearrange("p (g e) -> p g e", e=I // G), AXIS_X, ALU.max)
         nc.vector.tensor_reduce(row_max[:], bundle[:], AXIS_X, ALU.max)
         nc.vector.scalar_tensor_tensor(
             result[:], row_max[:].unsqueeze(2).to_broadcast([P, 2, G]), -0.5, bundle[:], ALU.mult, ALU.add

@@ -50,7 +50,7 @@ def tile_list_scores_gaps_listed_bundles_kernel(tc, xf, fk, ky_words, ky_scales,
             nc.sync.dma_start(out=planes[a][t][:], in_=xf_planes[a, t])
 
         def load_scale_rows(q):
-            nc.sync.dma_start(
+            nc.scalar.dma_start(
                 out=key_scales[32 * q : 32 * q + 4, :].bitcast(I32).rearrange("r (a c) -> r a c", a=PASSES),
                 in_=ky_scales[:, 4 * q : 4 * q + 4, :].bitcast(I32).rearrange("a r c -> r a c"),
             )
@@ -58,30 +58,28 @@ def tile_list_scores_gaps_listed_bundles_kernel(tc, xf, fk, ky_words, ky_scales,
         def load_words(a):
             nc.sync.dma_start(out=key_words[a][:], in_=ky_words[a].rearrange("p n t -> p (n t)").bitcast(I32))
 
+        nc.gpsimd.memset(key_scales[:].bitcast(I32), 0)
+        fk_rows = fk.rearrange("(a p t) o -> a p (t o)", a=PASSES, t=PACK)
+        for q in range(4):
+            load_scale_rows(q)
         warm = tile([P, 1], F32, "warm")
         nc.vector.memset(warm[:], 0.0)
         warm2 = tile([P, 1], F32, "warm2")
         nc.scalar.activation(warm2[:], warm[:], COPY)
-        nc.vector.memset(key_scales[:].bitcast(I32), 0)
-        fk_rows = fk.rearrange("(a p t) o -> a p (t o)", a=PASSES, t=PACK)
+        nc.gpsimd.dma_start(out=factor[0][0][:], in_=fk_rows[0][:, 0:2])
+        nc.gpsimd.dma_start(out=bias_col[:], in_=bi.rearrange("o (p c) -> p (o c)", c=2))
         make_identity(nc, ident[:])
 
-        load_plane(0, 0)
+        nc.sync.dma_start(list3[:], offs3)
         nc.sync.dma_start(list2[:], offs2)
+        load_plane(0, 0)
         nc.sync.dma_start(list1[:], offs)
         load_plane(0, 1)
-        nc.sync.dma_start(out=bias_col[:], in_=bi.rearrange("o (p c) -> p (o c)", c=2))
-        load_scale_rows(0)
-        load_scale_rows(1)
         load_plane(0, 2)
-        nc.sync.dma_start(list3[:], offs3)
-        load_scale_rows(2)
-        load_scale_rows(3)
         load_plane(0, 3)
-        nc.sync.dma_start(out=factor[0][0][:], in_=fk_rows[0][:, 0:2])
         load_plane(1, 0)
-        nc.sync.dma_start(out=factor[0][1][:], in_=fk_rows[0][:, 2:4])
         load_plane(1, 1)
+        nc.sync.dma_start(out=factor[0][1][:], in_=fk_rows[0][:, 2:4])
         load_plane(1, 2)
         nc.sync.dma_start(out=factor[1][0][:], in_=fk_rows[1][:, 0:2])
         load_plane(1, 3)
@@ -153,20 +151,20 @@ def tile_list_scores_gaps_listed_bundles_kernel(tc, xf, fk, ky_words, ky_scales,
         def gather_words(a):
             nc.vector.tensor_copy(k_codes[a][:], key_words[a][:].bitcast(U32).indirect(list3[:]))
 
-        d00 = gap(0, 0, 0, J, "vector")
-        nc.scalar.copy(out=bias[:].rearrange("m (p c) -> m p c", c=2), in_=bias_ps[:].rearrange("m c p -> m p c"))
-        d01 = gap(0, 1, 0, J)
         for a in range(PASSES):
             nc.vector.tensor_copy(k_scales[a][:], key_scales[:, a * V : (a + 1) * V].indirect(list3[:]))
+        d00 = gap(0, 0, 0, J, "vector")
+        nc.vector.tensor_copy(out=bias[:].rearrange("m (p c) -> m p c", c=2), in_=bias_ps[:].rearrange("m c p -> m p c"))
+        d01 = gap(0, 1, 0, J)
         scale_on_vector(0, 0, d00)
-        d02 = gap(0, 2, 0, J, "scalar")
+        d02 = gap(0, 2, 0, J)
         scale_on_vector(0, 1, d01)
         d03 = gap(0, 3, 0, J)
         d10 = gap(1, 0, 0, J)
+        d11 = gap(1, 1, 0, J)
         scale_on_scalar(0, 2, d02, 0, J)
         scale_on_scalar(0, 3, d03, 0, J)
         quantise(0, weave(nc.vector.tensor_copy, 0, 0, J), 0, J)
-        d11 = gap(1, 1, 0, J)
         d12 = gap(1, 2, 0, J)
         scale_on_scalar(1, 0, d10, 0, J)
         scale_on_scalar(1, 1, d11, 0, J)

@@ -62,10 +62,6 @@ def tile_list_scores_gaps_listed_bundles_kernel(tc, xf, fk, ky_words, ky_scales,
         fk_rows = fk.rearrange("(a p t) o -> a p (t o)", a=PASSES, t=PACK)
         for q in range(4):
             load_scale_rows(q)
-        warm = tile([P, 1], F32, "warm")
-        nc.vector.memset(warm[:], 0.0)
-        warm2 = tile([P, 1], F32, "warm2")
-        nc.scalar.activation(warm2[:], warm[:], COPY)
         nc.gpsimd.dma_start(out=factor[0][0][:], in_=fk_rows[0][:, 0:2])
         nc.gpsimd.dma_start(out=bias_col[:], in_=bi.rearrange("o (p c) -> p (o c)", c=2))
         make_identity(nc, ident[:])

from contextlib import ExitStack

import concourse.mybir as mybir
from concourse.masks import make_identity

K, T, J, I, V, G = 1024, 1024, 256, 256, 1024, 32
FLOPS = 2 * K * J * I

F32 = mybir.dt.float32
BF16 = mybir.dt.bfloat16
I32 = mybir.dt.int32
U32 = mybir.dt.uint32
U16 = mybir.dt.uint16
U8 = mybir.dt.uint8
E5M2X4 = mybir.dt.float8_e5m2_x4
ALU = mybir.AluOpType
COPY = mybir.ActivationFunctionType.Copy
AXIS_X = mybir.AxisListType.X

P = 128
PACK = 4
PASSES = K // (P * PACK)
HALF = 128
LIST_COLS = HALF // 16


def tile_list_scores_gaps_listed_bundles_kernel(tc, xf, fk, ky_words, ky_scales, bi, offs, offs2, offs3, out):
    nc = tc.nc
    with ExitStack() as ctx:
        keep = ctx.enter_context(tc.tile_pool(name="keep", bufs=1))
        psum = ctx.enter_context(tc.psum_pool(name="psum", bufs=1))

        def tile(shape, dtype, name):
            return keep.tile(shape, dtype, name=name, align_bytes=64)

        list1 = keep.tile([P, J // 16], U16, name="list1")
        list2 = keep.tile([P, J // 16], U16, name="list2")
        list3 = keep.tile([P, I // 16], U16, name="list3")
        planes = [[tile([P, T], F32, f"x{a}{t}") for t in range(PACK)] for a in range(PASSES)]
        key_words = [tile([P, V], I32, f"kw{a}") for a in range(PASSES)]
        key_scales = tile([P, PASSES * V], U8, "ks")
        factor = [[tile([P, 2], F32, f"factor{a}{u}") for u in range(2)] for a in range(PASSES)]
        bias_col = tile([P, 2], F32, "bias_col")
        ident = tile([P, P], F32, "ident")
        bias = tile([P, I], F32, "bias")

        xf_planes = xf.rearrange("(a p t) c -> a t p c", a=PASSES, t=PACK)

        def load_plane(a, t):
            nc.sync.dma_start(out=planes[a][t][:], in_=xf_planes[a, t])

        def load_scale_rows(q):
            nc.scalar.dma_start(
                out=key_scales[32 * q : 32 * q + 4, :].bitcast(I32).rearrange("r (a c) -> r a c", a=PASSES),
                in_=ky_scales[:, 4 * q : 4 * q + 4, :].bitcast(I32).rearrange("a r c -> r a c"),
            )

        def load_words(a):
            nc.sync.dma_start(out=key_words[a][:], in_=ky_words[a].rearrange("p n t -> p (n t)").bitcast(I32))

        nc.gpsimd.memset(key_scales[:].bitcast(I32), 0)
        fk_rows = fk.rearrange("(a p t) o -> a p (t o)", a=PASSES, t=PACK)
        for q in range(4):
            load_scale_rows(q)
        nc.gpsimd.dma_start(out=factor[0][0][:], in_=fk_rows[0][:, 0:2])
        nc.gpsimd.dma_start(out=bias_col[:], in_=bi.rearrange("o (p c) -> p (o c)", c=2))
        make_identity(nc, ident[:])

        nc.sync.dma_start(list3[:], offs3)
        nc.sync.dma_start(list2[:], offs2)
        load_plane(0, 0)
        nc.sync.dma_start(list1[:], offs)
        load_plane(0, 1)
        load_plane(0, 2)
        load_plane(0, 3)
        load_plane(1, 0)
        load_plane(1, 1)
        nc.sync.dma_start(out=factor[0][1][:], in_=fk_rows[0][:, 2:4])
        load_plane(1, 2)
        nc.sync.dma_start(out=factor[1][0][:], in_=fk_rows[1][:, 0:2])
        load_plane(1, 3)
        load_words(0)
        nc.sync.dma_start(out=factor[1][1][:], in_=fk_rows[1][:, 2:4])
        load_words(1)

        bias_ps = psum.tile([P, 2, P], F32, name="bias_ps")
        for c in range(2):
            nc.tensor.transpose(bias_ps[:, c, :], bias_col[:, c : c + 1].to_broadcast([P, P]), ident[:])

        flat = [tile([P, PACK, J], BF16, f"flat{a}") for a in range(PASSES)]
        u_codes = [tile([P, J], U32, f"uc{a}") for a in range(PASSES)]
        u_scales = [tile([P, J], U8, f"us{a}") for a in range(PASSES)]
        k_codes = [tile([P, I], U32, f"kc{a}") for a in range(PASSES)]
        k_scales = [tile([P, I], U8, f"ksg{a}") for a in range(PASSES)]
        acc = [psum.tile([P, I], F32, name=f"acc{h}") for h in range(2)]

        def gap(a, t, j0, n, first_on=None):
            second = tile([P, n], F32, f"second{a}{t}{j0}")
            diff = tile([P, n], F32, f"diff{a}{t}{j0}")
            cols = slice(j0 // 16, (j0 + n) // 16)
            window = planes[a][t][:]
            nc.scalar.activation(second[:], window.indirect(list2[:, cols]), COPY)
            if first_on is None:
                nc.vector.tensor_tensor(diff[:], window.indirect(list1[:, cols]), second[:], ALU.subtract)
                return diff
            first = tile([P, n], F32, f"first{a}{t}{j0}")
            if first_on == "vector":
                nc.vector.tensor_copy(first[:], window.indirect(list1[:, cols]))
            else:
                nc.scalar.activation(first[:], window.indirect(list1[:, cols]), COPY)
            nc.vector.tensor_tensor(diff[:], first[:], second[:], ALU.subtract)
            return diff

        def scale_on_vector(a, t, diff):
            nc.vector.tensor_scalar(flat[a][:, t, :], diff[:], factor[a][t // 2][:, t % 2 : t % 2 + 1], None, ALU.mult)

        def scale_on_scalar(a, t, diff, j0, n):
            nc.scalar.activation(flat[a][:, t, j0 : j0 + n], diff[:], COPY, scale=factor[a][t // 2][:, t % 2 : t % 2 + 1])

        def weave(copy, a, j0, n):
            woven = tile([P, n, PACK], BF16, f"woven{a}{j0}")
            copy(
                out=woven[:].rearrange("p (c i) t -> p c t i", i=4),
                in_=flat[a][:, :, j0 : j0 + n].rearrange("p t (c i) -> p c t i", i=4),
            )
            return woven

        def quantise(a, woven, j0, n):
            nc.vector.quantize_mx(
                out=u_codes[a][:, j0 : j0 + n].bitcast(E5M2X4),
                scales=u_scales[a][:, j0 : j0 + n],
                in_=woven[:].rearrange("p j t -> p (j t)"),
            )

        def multiply(a, jh):
            rows = slice(jh * HALF, (jh + 1) * HALF)
            nc.tensor.matmul_mx(
                out=acc[jh][:],
                lhsT=u_codes[a][:, rows].bitcast(E5M2X4),
                lhsT_scale=u_scales[a][:, rows],
                rhs=k_codes[a][:].bitcast(E5M2X4),
                rhs_scale=k_scales[a][:],
                start=(a == 0),
                stop=(a == PASSES - 1),
            )

        def gather_words(a):
            nc.vector.tensor_copy(k_codes[a][:], key_words[a][:].bitcast(U32).indirect(list3[:]))

        for a in range(PASSES):
            nc.vector.tensor_copy(k_scales[a][:], key_scales[:, a * V : (a + 1) * V].indirect(list3[:]))
        d00 = gap(0, 0, 0, J, "vector")
        nc.vector.tensor_copy(out=bias[:].rearrange("m (p c) -> m p c", c=2), in_=bias_ps[:].rearrange("m c p -> m p c"))
        d01 = gap(0, 1, 0, J)
        scale_on_vector(0, 0, d00)
        d02 = gap(0, 2, 0, J)
        scale_on_vector(0, 1, d01)
        d03 = gap(0, 3, 0, J)
        d10 = gap(1, 0, 0, J)
        d11 = gap(1, 1, 0, J)
        scale_on_scalar(0, 2, d02, 0, J)
        scale_on_scalar(0, 3, d03, 0, J)
        quantise(0, weave(nc.vector.tensor_copy, 0, 0, J), 0, J)
        d12 = gap(1, 2, 0, J)
        scale_on_scalar(1, 0, d10, 0, J)
        scale_on_scalar(1, 1, d11, 0, J)
        d13 = [gap(1, 3, jh * HALF, HALF) for jh in range(2)]
        scale_on_scalar(1, 2, d12, 0, J)
        for jh in range(2):
            scale_on_scalar(1, 3, d13[jh], jh * HALF, HALF)
        gather_words(0)
        for jh in range(2):
            multiply(0, jh)
        woven1 = [weave(nc.vector.tensor_copy, 1, 0, HALF), weave(nc.scalar.copy, 1, HALF, HALF)]
        gather_words(1)
        for jh in range(2):
            quantise(1, woven1[jh], jh * HALF, HALF)
            multiply(1, jh)

        scores = [tile([P, I], F32, f"scores{h}") for h in range(2)]
        bundle = tile([P, 2, G], F32, "bundle")
        row_max = tile([P, 2], F32, "row_max")
        result = tile([P, 2, G], F32, "result")
        for jh in range(2):
            nc.vector.tensor_tensor(scores[jh][:], acc[jh][:], bias[:], ALU.add)
        for jh in range(2):
            nc.vector.tensor_reduce(bundle[:, jh, :], scores[jh][:].rearrange("p (g e) -> p g e", e=I // G), AXIS_X, ALU.max)
        nc.vector.tensor_reduce(row_max[:], bundle[:], AXIS_X, ALU.max)
        nc.vector.scalar_tensor_tensor(
            result[:], row_max[:].unsqueeze(2).to_broadcast([P, 2, G]), -0.5, bundle[:], ALU.mult, ALU.add
        )
        nc.sync.dma_start(out=out.rearrange("(h p) g -> p h g", p=P), in_=result[:])
